import numpy as np
import ml_dtypes


def mxq(x, axis, fmt="e4m3"):
    dtype, down = {"e4m3": (ml_dtypes.float8_e4m3fn, 7), "e5m2": (ml_dtypes.float8_e5m2, 14)}[fmt]
    v = np.moveaxis(np.asarray(x, np.float32).astype(ml_dtypes.bfloat16).astype(np.float64), axis, -1)
    blocks = v.reshape(v.shape[:-1] + (-1, 32))
    amax = np.abs(blocks).max(-1, keepdims=True)
    byte = np.maximum(np.where(amax > 0, np.frexp(amax)[1] - 1 + 127, 0) - down, 1)
    scale = np.exp2(byte - 127.0)
    codes = (blocks / scale).astype(np.float32).astype(dtype).astype(np.float64)
    return np.moveaxis((codes * scale).reshape(v.shape), -1, axis)


WIDE = False


def mx_kscale(k):
    if not WIDE:
        return np.ones(k)
    levels = np.array([10, -10, 5, -5, 0])
    if k % 512:
        return np.exp2(np.random.permutation(np.resize(levels, k // 32))).repeat(32)
    a = np.empty((k // 512, 16))
    for p in range(k // 512):
        a[p, :8] = np.random.permutation(np.resize(levels, 8))
        for g in range(8):
            far = levels[np.abs(levels - a[p, g]) >= 10]
            a[p, g + 8] = far[np.random.randint(len(far))]
    return np.exp2(a.ravel()).repeat(32)


def f64(x):
    return np.asarray(x).astype(np.float64)


def striped(idx):
    return np.tile(idx.reshape(-1, 16).T, (8, 1)).astype(np.uint16)


def unstriped(offs):
    return offs[:16].T.reshape(-1).astype(np.int64)


E2M1 = np.array([0.0, 0.5, 1.0, 1.5, 2.0, 3.0, 4.0, 6.0, -0.0, -0.5, -1.0, -1.5, -2.0, -3.0, -4.0, -6.0])


def pack_weight(w, fmt):
    k, n = w.shape
    w = f64(np.asarray(w, np.float32).astype(ml_dtypes.bfloat16)).reshape(k // 32, 32, n)
    amax = np.abs(w).max(1)
    if fmt == "e4m3":
        byte = np.frexp(amax)[1] - 1 + 127 - 7
    else:
        mant, ex = np.frexp(amax / 6.0)
        byte = np.where(mant > 0.5, ex, ex - 1) + 127
    byte = np.clip(np.where(amax > 0, byte, 1), 1, 254)
    scaled = (w * np.exp2(127.0 - byte)[:, None, :]).reshape(k, n).astype(np.float32)
    by_word = np.ascontiguousarray(scaled.reshape(k // 512, 128, 4, n).transpose(0, 1, 3, 2))
    if fmt == "e4m3":
        words = by_word.astype(ml_dtypes.float8_e4m3fn).view(np.uint8)
    else:
        c = by_word.astype(ml_dtypes.float4_e2m1fn).view(np.uint8) & 0xF
        words = (c[..., 0::2] | (c[..., 1::2] << 4)).reshape(k // 512, 128, 2 * n)
    return np.ascontiguousarray(words), np.ascontiguousarray(byte.astype(np.uint8).reshape(k // 512, 16, n))


def unpack_weight(words, scales, fmt):
    g, _, n = scales.shape
    words = np.ascontiguousarray(words).reshape(g, 128, n, -1)
    if fmt == "e4m3":
        vals = words.view(ml_dtypes.float8_e4m3fn).astype(np.float64)
    else:
        nib = np.empty((g, 128, n, 4), np.uint8)
        nib[..., 0::2] = words & 0xF
        nib[..., 1::2] = words >> 4
        vals = E2M1[nib]
    vals = vals * np.repeat(np.exp2(scales.astype(np.float64) - 127.0), 8, axis=1)[..., None]
    return vals.transpose(0, 1, 3, 2).reshape(g * 512, n)


def pack_table(v):
    words, scales = pack_weight(v, "e4m3")
    return np.concatenate([words.reshape(words.shape[0], -1), scales.reshape(scales.shape[0], -1)], axis=1)


def unpack_table(tab):
    g, t = tab.shape[0], tab.shape[1] // 528
    return unpack_weight(tab[:, :512 * t].reshape(g, 128, t, 4), tab[:, 512 * t:].reshape(g, 16, t), "e4m3")


K, M, T, S = 1536, 128, 4096, 1536


def setup_inputs():
    n = np.random.standard_normal
    s = mx_kscale(K)[:, None]
    return {
        "tab": pack_table(n((K, T)) * s),
        "w": (n((K, M)) / np.sqrt(K) / s).astype(np.float32),
        "b": (0.3 * n(128)).astype(np.float32),
        "offs": striped(np.random.permutation(T)[:S]),
    }


def reference(tab, w, b, offs):
    tab_ = unpack_table(tab)[:, unstriped(offs)]
    w_ = mxq(f64(w), 0, "e4m3")
    y = w_.T @ tab_
    return y + f64(b)[:, None]

@@ -1,0 +1,122 @@
+import concourse.mybir as mybir
+
+K, M, T, S = 1536, 128, 4096, 1536
+FLOPS = 2 * K * M * S
+
+F32 = mybir.dt.float32
+BF16 = mybir.dt.bfloat16
+I32 = mybir.dt.int32
+U32 = mybir.dt.uint32
+U16 = mybir.dt.uint16
+U8 = mybir.dt.uint8
+FP8X4 = mybir.dt.float8_e4m3fn_x4
+IDENTITY = mybir.ActivationFunctionType.Identity
+ADD = mybir.AluOpType.add
+
+P = 128
+PASSES = K // 512
+
+
+def tile_list_tabw_bias_kernel(tc, tab, w, b, offs, out):
+    nc = tc.nc
+    with (
+        tc.tile_pool(name="lists", bufs=1) as lists,
+        tc.tile_pool(name="keep", bufs=1) as keep,
+        tc.psum_pool(name="psum", bufs=1) as psum,
+    ):
+        offsets = lists.tile([P, S // 16], U16, name="offsets")
+        words = [keep.tile([P, T], I32, name=f"words{a}", align_bytes=64) for a in range(PASSES)]
+        scales = keep.tile([P, T // 4], I32, name="scales", align_bytes=64)
+        picked = [keep.tile([P, S], U32, name=f"picked{a}", align_bytes=64) for a in range(PASSES)]
+        picked_scales = keep.tile([P, S], U8, name="picked_scales", align_bytes=64)
+        w_raw = [keep.tile([P, 4, M], F32, name=f"w_raw{a}", align_bytes=64) for a in range(PASSES)]
+        w_bf = [keep.tile([P, M, 4], BF16, name=f"w_bf{a}", align_bytes=64) for a in range(PASSES)]
+        w_codes = [keep.tile([P, M], U32, name=f"w_codes{a}", align_bytes=64) for a in range(PASSES)]
+        w_scales = [keep.tile([P, M], U8, name=f"w_scales{a}", align_bytes=64) for a in range(PASSES)]
+        bias = keep.tile([P, 1], F32, name="bias")
+
+        def load_words(a):
+            nc.sync.dma_start(
+                words[a][:],
+                tab[a, 0 : 512 * T].bitcast(I32).rearrange("(p t) -> p t", p=P),
+            )
+
+        def load_w(a):
+            nc.sync.dma_start(
+                w_raw[a][:], w[512 * a : 512 * (a + 1), :].rearrange("(p j) n -> p j n", j=4)
+            )
+
+        nc.vector.memset(scales[:], 0)
+        nc.sync.dma_start(offsets[:], offs)
+        load_words(0)
+        scale_rows = tab[:, 512 * T : 528 * T].bitcast(I32).rearrange("a (q t) -> a q t", q=16)
+        for quad in range(4):
+            nc.gpsimd.dma_start(
+                scales[32 * quad : 32 * quad + 12, :], scale_rows[:, 4 * quad : 4 * quad + 4, :]
+            )
+        nc.scalar.dma_start(bias[:], b.rearrange("(n one) -> n one", one=1))
+        for a in range(PASSES):
+            load_w(a)
+        load_words(1)
+        load_words(2)
+
+        def pick_words(a, j0, j1):
+            nc.vector.tensor_copy(
+                picked[a][:, j0:j1],
+                words[a][:].bitcast(U32).indirect(offsets[:, j0 // 16 : j1 // 16]),
+            )
+
+        def quantise_w(a):
+            nc.scalar.copy(w_bf[a][:], w_raw[a][:].rearrange("p j n -> p n j"))
+            nc.vector.quantize_mx(
+                out=w_codes[a][:].bitcast(FP8X4),
+                scales=w_scales[a][:],
+                in_=w_bf[a][:].rearrange("p n j -> p (n j)"),
+            )
+
+        pieces = [(0, 512), (512, 1024), (1024, 1280), (1280, 1536)]
+        accs = [psum.tile([M, j1 - j0], F32, name=f"acc{j0}") for j0, j1 in pieces]
+
+        def multiply(a, i):
+            j0, j1 = pieces[i]
+            nc.tensor.matmul_mx(
+                out=accs[i][:],
+                lhsT=w_codes[a][:].bitcast(FP8X4),
+                lhsT_scale=w_scales[a][:],
+                rhs=picked[a][:, j0:j1].bitcast(FP8X4),
+                rhs_scale=picked_scales[4 * a : P, j0:j1],
+                start=(a == 0),
+                stop=(a == PASSES - 1),
+            )
+
+        pick_words(0, 0, S)
+        nc.vector.tensor_copy(picked_scales[:], scales[:].bitcast(U8).indirect(offsets[:]))
+        for a in range(PASSES):
+            quantise_w(a)
+        for i in range(4):
+            multiply(0, i)
+        pick_words(1, 0, S)
+        for i in range(4):
+            multiply(1, i)
+
+        results = [keep.tile([M, j1 - j0], F32, name=f"result{j0}") for j0, j1 in pieces]
+
+        def finish(i, on_vector, queue):
+            j0, j1 = pieces[i]
+            if on_vector:
+                nc.vector.tensor_scalar(results[i][:], accs[i][:], bias[:], None, op0=ADD)
+            else:
+                nc.scalar.activation(results[i][:], accs[i][:], IDENTITY, bias=bias[:])
+            queue.dma_start(out[:, j0:j1], results[i][:])
+
+        pick_words(2, 0, 512)
+        multiply(2, 0)
+        finish(0, False, nc.sync)
+        pick_words(2, 512, 1024)
+        multiply(2, 1)
+        finish(1, False, nc.sync)
+        pick_words(2, 1024, S)
+        multiply(2, 2)
+        multiply(2, 3)
+        finish(2, False, nc.scalar)
+        finish(3, True, nc.sync)

@@ -26,13 +26,13 @@ def tile_list_tabw_bias_kernel(tc, tab, w, b, offs, out):
     ):
         offsets = lists.tile([P, S // 16], U16, name="offsets")
         words = [keep.tile([P, T], I32, name=f"words{a}", align_bytes=64) for a in range(PASSES)]
-        scales = keep.tile([P, T // 4], I32, name="scales", align_bytes=64)
-        picked = [keep.tile([P, S], U32, name=f"picked{a}", align_bytes=64) for a in range(PASSES)]
+        scales = keep.tile([P, T // 4], I32, name="scales", tag="shared", align_bytes=64)
         picked_scales = keep.tile([P, S], U8, name="picked_scales", align_bytes=64)
-        w_raw = [keep.tile([P, 4, M], F32, name=f"w_raw{a}", align_bytes=64) for a in range(PASSES)]
-        w_bf = [keep.tile([P, M, 4], BF16, name=f"w_bf{a}", align_bytes=64) for a in range(PASSES)]
-        w_codes = [keep.tile([P, M], U32, name=f"w_codes{a}", align_bytes=64) for a in range(PASSES)]
-        w_scales = [keep.tile([P, M], U8, name=f"w_scales{a}", align_bytes=64) for a in range(PASSES)]
+        w_raw = keep.tile([P, PASSES, 4, M], F32, name="w_raw", align_bytes=64)
+        w_bf = keep.tile([P, PASSES, M, 4], BF16, name="w_bf", align_bytes=64)
+        w_codes = keep.tile([P, PASSES * M], U32, name="w_codes", align_bytes=64)
+        w_scales = keep.tile([P, PASSES * M], U8, name="w_scales", align_bytes=64)
+        b_raw = keep.tile([P, 1], F32, name="b_raw")
         bias = keep.tile([P, 1], F32, name="bias")
 
         def load_words(a):
@@ -41,24 +41,31 @@ def tile_list_tabw_bias_kernel(tc, tab, w, b, offs, out):
                 tab[a, 0 : 512 * T].bitcast(I32).rearrange("(p t) -> p t", p=P),
             )
 
-        def load_w(a):
+        def load_w(a0, a1):
             nc.sync.dma_start(
-                w_raw[a][:], w[512 * a : 512 * (a + 1), :].rearrange("(p j) n -> p j n", j=4)
+                w_raw[:, a0:a1].rearrange("p a j n -> p a (j n)"),
+                w[512 * a0 : 512 * a1, :].rearrange("(a p j) n -> p a (j n)", p=P, j=4),
             )
 
-        nc.vector.memset(scales[:], 0)
-        nc.sync.dma_start(offsets[:], offs)
-        load_words(0)
         scale_rows = tab[:, 512 * T : 528 * T].bitcast(I32).rearrange("a (q t) -> a q t", q=16)
+
+        nc.vector.memset(scales[:], 0)
+        nc.vector.memset(words[0][:, 0:8], 0)
+        nc.sync.dma_start(offsets[:], offs)
         for quad in range(4):
-            nc.gpsimd.dma_start(
+            queue = nc.sync if quad % 2 == 0 else nc.scalar
+            queue.dma_start(
                 scales[32 * quad : 32 * quad + 12, :], scale_rows[:, 4 * quad : 4 * quad + 4, :]
             )
-        nc.scalar.dma_start(bias[:], b.rearrange("(n one) -> n one", one=1))
-        for a in range(PASSES):
-            load_w(a)
+        nc.scalar.dma_start(b_raw[:], b.rearrange("(n one) -> n one", one=1))
+        nc.scalar.activation(bias[:], b_raw[:], IDENTITY)
+        load_words(0)
         load_words(1)
+        load_w(0, 2)
+        load_w(2, 3)
         load_words(2)
+
+        picked = []
 
         def pick_words(a, j0, j1):
             nc.vector.tensor_copy(
@@ -66,12 +73,14 @@ def tile_list_tabw_bias_kernel(tc, tab, w, b, offs, out):
                 words[a][:].bitcast(U32).indirect(offsets[:, j0 // 16 : j1 // 16]),
             )
 
-        def quantise_w(a):
-            nc.scalar.copy(w_bf[a][:], w_raw[a][:].rearrange("p j n -> p n j"))
+        def round_w(a):
+            nc.scalar.copy(w_bf[:, a], w_raw[:, a].rearrange("p j n -> p n j"))
+
+        def quantise_w(a0, a1):
             nc.vector.quantize_mx(
-                out=w_codes[a][:].bitcast(FP8X4),
-                scales=w_scales[a][:],
-                in_=w_bf[a][:].rearrange("p n j -> p (n j)"),
+                out=w_codes[:, M * a0 : M * a1].bitcast(FP8X4),
+                scales=w_scales[:, M * a0 : M * a1],
+                in_=w_bf[:, a0:a1].rearrange("p a n j -> p (a n j)"),
             )
 
         pieces = [(0, 512), (512, 1024), (1024, 1280), (1280, 1536)]
@@ -81,23 +90,13 @@ def tile_list_tabw_bias_kernel(tc, tab, w, b, offs, out):
             j0, j1 = pieces[i]
             nc.tensor.matmul_mx(
                 out=accs[i][:],
-                lhsT=w_codes[a][:].bitcast(FP8X4),
-                lhsT_scale=w_scales[a][:],
+                lhsT=w_codes[:, M * a : M * (a + 1)].bitcast(FP8X4),
+                lhsT_scale=w_scales[:, M * a : M * (a + 1)],
                 rhs=picked[a][:, j0:j1].bitcast(FP8X4),
                 rhs_scale=picked_scales[4 * a : P, j0:j1],
                 start=(a == 0),
                 stop=(a == PASSES - 1),
             )
-
-        pick_words(0, 0, S)
-        nc.vector.tensor_copy(picked_scales[:], scales[:].bitcast(U8).indirect(offsets[:]))
-        for a in range(PASSES):
-            quantise_w(a)
-        for i in range(4):
-            multiply(0, i)
-        pick_words(1, 0, S)
-        for i in range(4):
-            multiply(1, i)
 
         results = [keep.tile([M, j1 - j0], F32, name=f"result{j0}") for j0, j1 in pieces]
 
@@ -109,6 +108,19 @@ def tile_list_tabw_bias_kernel(tc, tab, w, b, offs, out):
                 nc.scalar.activation(results[i][:], accs[i][:], IDENTITY, bias=bias[:])
             queue.dma_start(out[:, j0:j1], results[i][:])
 
+        nc.vector.tensor_copy(picked_scales[:], scales[:].bitcast(U8).indirect(offsets[:]))
+        picked.append(keep.tile([P, S], U32, name="picked0", tag="shared", align_bytes=64))
+        pick_words(0, 0, S)
+        for a in range(1, PASSES):
+            picked.append(keep.tile([P, S], U32, name=f"picked{a}", align_bytes=64))
+        pick_words(1, 0, S)
+        for a in range(PASSES):
+            round_w(a)
+        quantise_w(0, 2)
+        quantise_w(2, 3)
+        for a in range(2):
+            for i in range(4):
+                multiply(a, i)
         pick_words(2, 0, 512)
         multiply(2, 0)
         finish(0, False, nc.sync)

@@ -28,7 +28,7 @@ def tile_list_tabw_bias_kernel(tc, tab, w, b, offs, out):
         words = [keep.tile([P, T], I32, name=f"words{a}", align_bytes=64) for a in range(PASSES)]
         scales = keep.tile([P, T // 4], I32, name="scales", tag="shared", align_bytes=64)
         picked_scales = keep.tile([P, S], U8, name="picked_scales", align_bytes=64)
-        w_raw = keep.tile([P, PASSES, 4, M], F32, name="w_raw", align_bytes=64)
+        w_raw = [keep.tile([P, 4, M], F32, name=f"w_raw{a}", align_bytes=64) for a in range(PASSES)]
         w_bf = keep.tile([P, PASSES, M, 4], BF16, name="w_bf", align_bytes=64)
         w_codes = keep.tile([P, PASSES * M], U32, name="w_codes", align_bytes=64)
         w_scales = keep.tile([P, PASSES * M], U8, name="w_scales", align_bytes=64)
@@ -41,28 +41,28 @@ def tile_list_tabw_bias_kernel(tc, tab, w, b, offs, out):
                 tab[a, 0 : 512 * T].bitcast(I32).rearrange("(p t) -> p t", p=P),
             )
 
-        def load_w(a0, a1):
+        def load_w(a):
             nc.sync.dma_start(
-                w_raw[:, a0:a1].rearrange("p a j n -> p a (j n)"),
-                w[512 * a0 : 512 * a1, :].rearrange("(a p j) n -> p a (j n)", p=P, j=4),
+                w_raw[a][:], w[512 * a : 512 * (a + 1), :].rearrange("(p j) n -> p j n", j=4)
             )
 
         scale_rows = tab[:, 512 * T : 528 * T].bitcast(I32).rearrange("a (q t) -> a q t", q=16)
 
         nc.vector.memset(scales[:], 0)
-        nc.vector.memset(words[0][:, 0:8], 0)
+        for a in range(PASSES):
+            nc.vector.memset(words[a][:, 0:8], 0)
         nc.sync.dma_start(offsets[:], offs)
+        for a in range(PASSES):
+            load_w(a)
         for quad in range(4):
             queue = nc.sync if quad % 2 == 0 else nc.scalar
             queue.dma_start(
                 scales[32 * quad : 32 * quad + 12, :], scale_rows[:, 4 * quad : 4 * quad + 4, :]
             )
+        load_words(0)
         nc.scalar.dma_start(b_raw[:], b.rearrange("(n one) -> n one", one=1))
         nc.scalar.activation(bias[:], b_raw[:], IDENTITY)
-        load_words(0)
         load_words(1)
-        load_w(0, 2)
-        load_w(2, 3)
         load_words(2)
 
         picked = []
@@ -74,7 +74,7 @@ def tile_list_tabw_bias_kernel(tc, tab, w, b, offs, out):
             )
 
         def round_w(a):
-            nc.scalar.copy(w_bf[:, a], w_raw[:, a].rearrange("p j n -> p n j"))
+            nc.vector.tensor_copy(w_bf[:, a], w_raw[a][:].rearrange("p j n -> p n j"))
 
         def quantise_w(a0, a1):
             nc.vector.quantize_mx(
@@ -108,17 +108,16 @@ def tile_list_tabw_bias_kernel(tc, tab, w, b, offs, out):
                 nc.scalar.activation(results[i][:], accs[i][:], IDENTITY, bias=bias[:])
             queue.dma_start(out[:, j0:j1], results[i][:])
 
-        nc.vector.tensor_copy(picked_scales[:], scales[:].bitcast(U8).indirect(offsets[:]))
-        picked.append(keep.tile([P, S], U32, name="picked0", tag="shared", align_bytes=64))
-        pick_words(0, 0, S)
-        for a in range(1, PASSES):
-            picked.append(keep.tile([P, S], U32, name=f"picked{a}", align_bytes=64))
-        pick_words(1, 0, S)
         for a in range(PASSES):
             round_w(a)
         quantise_w(0, 2)
         quantise_w(2, 3)
+        nc.vector.tensor_copy(picked_scales[:], scales[:].bitcast(U8).indirect(offsets[:]))
+        picked.append(keep.tile([P, S], U32, name="picked0", tag="shared", align_bytes=64))
+        for a in range(1, PASSES):
+            picked.append(keep.tile([P, S], U32, name=f"picked{a}", align_bytes=64))
         for a in range(2):
+            pick_words(a, 0, S)
             for i in range(4):
                 multiply(a, i)
         pick_words(2, 0, 512)

import concourse.mybir as mybir

K, M, T, S = 1536, 128, 4096, 1536
FLOPS = 2 * K * M * S

F32 = mybir.dt.float32
BF16 = mybir.dt.bfloat16
I32 = mybir.dt.int32
U32 = mybir.dt.uint32
U16 = mybir.dt.uint16
U8 = mybir.dt.uint8
FP8X4 = mybir.dt.float8_e4m3fn_x4
IDENTITY = mybir.ActivationFunctionType.Identity
ADD = mybir.AluOpType.add

P = 128
PASSES = K // 512


def tile_list_tabw_bias_kernel(tc, tab, w, b, offs, out):
    nc = tc.nc
    with (
        tc.tile_pool(name="lists", bufs=1) as lists,
        tc.tile_pool(name="keep", bufs=1) as keep,
        tc.psum_pool(name="psum", bufs=1) as psum,
    ):
        offsets = lists.tile([P, S // 16], U16, name="offsets")
        words = [keep.tile([P, T], I32, name=f"words{a}", align_bytes=64) for a in range(PASSES)]
        scales = keep.tile([P, T // 4], I32, name="scales", tag="shared", align_bytes=64)
        picked_scales = keep.tile([P, S], U8, name="picked_scales", align_bytes=64)
        w_raw = [keep.tile([P, 4, M], F32, name=f"w_raw{a}", align_bytes=64) for a in range(PASSES)]
        w_bf = keep.tile([P, PASSES, M, 4], BF16, name="w_bf", align_bytes=64)
        w_codes = keep.tile([P, PASSES * M], U32, name="w_codes", align_bytes=64)
        w_scales = keep.tile([P, PASSES * M], U8, name="w_scales", align_bytes=64)
        b_raw = keep.tile([P, 1], F32, name="b_raw")
        bias = keep.tile([P, 1], F32, name="bias")

        def load_words(a):
            nc.sync.dma_start(
                words[a][:],
                tab[a, 0 : 512 * T].bitcast(I32).rearrange("(p t) -> p t", p=P),
            )

        def load_w(a):
            nc.sync.dma_start(
                w_raw[a][:], w[512 * a : 512 * (a + 1), :].rearrange("(p j) n -> p j n", j=4)
            )

        scale_rows = tab[:, 512 * T : 528 * T].bitcast(I32).rearrange("a (q t) -> a q t", q=16)

        nc.vector.memset(scales[:], 0)
        for a in range(PASSES):
            nc.vector.memset(words[a][:, 0:8], 0)
        nc.sync.dma_start(offsets[:], offs)
        for a in range(PASSES):
            load_w(a)
        for quad in range(4):
            queue = nc.sync if quad % 2 == 0 else nc.scalar
            queue.dma_start(
                scales[32 * quad : 32 * quad + 12, :], scale_rows[:, 4 * quad : 4 * quad + 4, :]
            )
        load_words(0)
        nc.scalar.dma_start(b_raw[:], b.rearrange("(n one) -> n one", one=1))
        nc.scalar.activation(bias[:], b_raw[:], IDENTITY)
        load_words(1)
        load_words(2)

        picked = []

        def pick_words(a, j0, j1):
            nc.vector.tensor_copy(
                picked[a][:, j0:j1],
                words[a][:].bitcast(U32).indirect(offsets[:, j0 // 16 : j1 // 16]),
            )

        def round_w(a):
            nc.vector.tensor_copy(w_bf[:, a], w_raw[a][:].rearrange("p j n -> p n j"))

        def quantise_w(a0, a1):
            nc.vector.quantize_mx(
                out=w_codes[:, M * a0 : M * a1].bitcast(FP8X4),
                scales=w_scales[:, M * a0 : M * a1],
                in_=w_bf[:, a0:a1].rearrange("p a n j -> p (a n j)"),
            )

        pieces = [(0, 512), (512, 1024), (1024, 1280), (1280, 1536)]
        accs = [psum.tile([M, j1 - j0], F32, name=f"acc{j0}") for j0, j1 in pieces]

        def multiply(a, i):
            j0, j1 = pieces[i]
            nc.tensor.matmul_mx(
                out=accs[i][:],
                lhsT=w_codes[:, M * a : M * (a + 1)].bitcast(FP8X4),
                lhsT_scale=w_scales[:, M * a : M * (a + 1)],
                rhs=picked[a][:, j0:j1].bitcast(FP8X4),
                rhs_scale=picked_scales[4 * a : P, j0:j1],
                start=(a == 0),
                stop=(a == PASSES - 1),
            )

        results = [keep.tile([M, j1 - j0], F32, name=f"result{j0}") for j0, j1 in pieces]

        def finish(i, on_vector, queue):
            j0, j1 = pieces[i]
            if on_vector:
                nc.vector.tensor_scalar(results[i][:], accs[i][:], bias[:], None, op0=ADD)
            else:
                nc.scalar.activation(results[i][:], accs[i][:], IDENTITY, bias=bias[:])
            queue.dma_start(out[:, j0:j1], results[i][:])

        for a in range(PASSES):
            round_w(a)
        quantise_w(0, 2)
        quantise_w(2, 3)
        nc.vector.tensor_copy(picked_scales[:], scales[:].bitcast(U8).indirect(offsets[:]))
        picked.append(keep.tile([P, S], U32, name="picked0", tag="shared", align_bytes=64))
        for a in range(1, PASSES):
            picked.append(keep.tile([P, S], U32, name=f"picked{a}", align_bytes=64))
        for a in range(2):
            pick_words(a, 0, S)
            for i in range(4):
                multiply(a, i)
        pick_words(2, 0, 512)
        multiply(2, 0)
        finish(0, False, nc.sync)
        pick_words(2, 512, 1024)
        multiply(2, 1)
        finish(1, False, nc.sync)
        pick_words(2, 1024, S)
        multiply(2, 2)
        multiply(2, 3)
        finish(2, False, nc.scalar)
        finish(3, True, nc.sync)
